import numpy as np
import ml_dtypes


def mxq(x, axis, fmt="e4m3"):
    dtype, down = {"e4m3": (ml_dtypes.float8_e4m3fn, 7), "e5m2": (ml_dtypes.float8_e5m2, 14)}[fmt]
    v = np.moveaxis(np.asarray(x, np.float32).astype(ml_dtypes.bfloat16).astype(np.float64), axis, -1)
    blocks = v.reshape(v.shape[:-1] + (-1, 32))
    amax = np.abs(blocks).max(-1, keepdims=True)
    byte = np.maximum(np.where(amax > 0, np.frexp(amax)[1] - 1 + 127, 0) - down, 1)
    scale = np.exp2(byte - 127.0)
    codes = (blocks / scale).astype(np.float32).astype(dtype).astype(np.float64)
    return np.moveaxis((codes * scale).reshape(v.shape), -1, axis)


WIDE = False


def mx_kscale(k, group=512):
    if not WIDE:
        return np.ones(k)
    levels = np.array([10, -10, 5, -5, 0])
    if group != 512:
        return np.exp2(np.random.permutation(np.resize(levels, k // group))).repeat(group)
    if k % 512:
        return np.exp2(np.random.permutation(np.resize(levels, k // 32))).repeat(32)
    a = np.empty((k // 512, 16))
    for p in range(k // 512):
        a[p, :8] = np.random.permutation(np.resize(levels, 8))
        for g in range(8):
            far = levels[np.abs(levels - a[p, g]) >= 10]
            a[p, g + 8] = far[np.random.randint(len(far))]
    return np.exp2(a.ravel()).repeat(32)


def f64(x):
    return np.asarray(x).astype(np.float64)


def striped(idx):
    return np.tile(np.asarray(idx).reshape(-1, 16).T, (8, 1)).astype(np.uint16)


def unstriped(offs):
    return offs[:16].T.reshape(-1).astype(np.int64)


H, KV, D, NQ, N = 4, 4, 128, 512, 512


def setup_inputs():
    n = np.random.standard_normal
    s = mx_kscale(D, 0)[:, None]
    u = mx_kscale(N)
    t = np.random.uniform(0.5, 2.0, N) * u
    v = n((KV, N, 128))
    v[:, :, 127] = 1.0
    return {
        "qT": (n((H, D, NQ)) * s * (0.70 / np.sqrt(D))).astype(np.float32),
        "kT": (n((KV, D, N)) / s).astype(np.float32),
        "t": t.reshape(N, 1).astype(np.float32),
        "v": (v / t[:, None]).astype(np.float32),
        "mask": (np.arange(N)[:, None] <= np.sort(np.random.randint(N // 4, N, NQ))[None, :]).astype(np.float32),
        "og": n((H, NQ, 128)).astype(np.float32),
    }


def reference(qT, kT, t, v, mask, og):
    a = mxq(f64(kT), 1, "e4m3").transpose(0, 2, 1) @ mxq(f64(qT), 1, "e4m3")
    p = np.exp(a)
    p = p * f64(mask)
    w = p * f64(t)
    y = mxq(w, 1, "e4m3").transpose(0, 2, 1) @ mxq(f64(v), 1, "e4m3")
    y = y / (y[:, :, 127:128])
    y = y / (1.0 + np.exp(-f64(og)))
    return y

@@ -1,0 +1,252 @@
+from contextlib import ExitStack
+
+import concourse.mybir as mybir
+
+H, D, NQ, N = 4, 128, 512, 512
+FLOPS = 2 * 2 * H * NQ * N * D
+
+F32 = mybir.dt.float32
+BF16 = mybir.dt.bfloat16
+U32 = mybir.dt.uint32
+U8 = mybir.dt.uint8
+FP8X4 = mybir.dt.float8_e4m3fn_x4
+ACT = mybir.ActivationFunctionType
+ALU = mybir.AluOpType
+
+P = 128
+PACK = 4
+ROWS = 32
+QT = 128
+NT = NQ // QT
+
+
+def tile_rows_mask_gate_kernel(tc, qT, kT, t, v, mask, og, out):
+    nc = tc.nc
+    q_src = qT.rearrange("g (p j) c -> (g p) j c", j=PACK)
+    k_src = kT.rearrange("g (p j) c -> (g p) j c", j=PACK)
+    v_src = v.rearrange("g (p r) e -> p g r e", r=PACK)
+    t_src = t.rearrange("(p r) o -> p (r o)", r=PACK)
+    mask_src = mask.rearrange("(p r) c -> p r c", r=PACK)
+    og_src = og.rearrange("g (b p) e -> b p g e", p=QT)
+    out_dst = out.rearrange("g (b p) e -> b p g e", p=QT)
+
+    with ExitStack() as ctx:
+        sb = ctx.enter_context(tc.tile_pool(name="sb", bufs=1))
+        ps = ctx.enter_context(tc.psum_pool(name="ps", bufs=1))
+        ctx.enter_context(tc.manual_schedule())
+
+        def tiles(name, count, shape, dtype):
+            return [sb.tile(shape, dtype, name="%s%d" % (name, i), align_bytes=64) for i in range(count)]
+
+        k_raw = tiles("k_raw", 2, [P, PACK, N // 2], F32)
+        q_raw = tiles("q_raw", 2, [P, PACK, QT], F32) + tiles("q_raw_late", 1, [P, PACK, 2 * QT], F32)
+        mask_raw = tiles("mask_raw", 2, [P, PACK, QT], F32) + tiles("mask_raw_late", 1, [P, PACK, 2 * QT], F32)
+        v_raw = tiles("v_raw", 2, [P, 2, PACK, D], F32)
+        og_raw = tiles("og_raw", NT, [P, H, D], F32)
+        t_sb = sb.tile([P, PACK], F32, name="t_sb", align_bytes=64)
+
+        k_bf = sb.tile([P, PACK, P, PACK], BF16, name="k_bf", align_bytes=64)
+        k_codes = sb.tile([P, N], U32, name="k_codes", align_bytes=64)
+        k_scales = sb.tile([P, N], U8, name="k_scales", align_bytes=64)
+        q_bf = tiles("q_bf", 2, [P, QT, PACK], BF16) + tiles("q_bf_late", 1, [P, 2 * QT, PACK], BF16)
+        q_codes = tiles("q_codes", 2, [P, QT], U32) + tiles("q_codes_late", 1, [P, 2 * QT], U32)
+        q_scales = tiles("q_scales", 2, [P, QT], U8) + tiles("q_scales_late", 1, [P, 2 * QT], U8)
+        v_bf = tiles("v_bf", 2, [P, 2, D, PACK], BF16)
+        v_codes = tiles("v_codes", 2, [P, 2 * D], U32)
+        v_scales = tiles("v_scales", 2, [P, 2 * D], U8)
+        mt = tiles("mt", NT, [P, QT, PACK], F32)
+        p_f = tiles("p_f", NT * H, [P, QT, PACK], F32)
+        w_bf = tiles("w_bf", NT * 2, [P, 2, QT * PACK], BF16)
+        w_codes = tiles("w_codes", NT * 2, [P, 2 * QT], U32)
+        w_scales = tiles("w_scales", NT * 2, [P, 2 * QT], U8)
+        gate = tiles("gate", NT, [P, H, D], F32)
+        rcp = tiles("rcp", NT, [P, H], F32)
+        res = tiles("res", NT, [P, H, D], F32)
+
+        score = [ps.tile([P, PACK, QT], F32, name="score%d" % g) for g in range(H)]
+        y = [ps.tile([P, H, D], F32, name="y%d" % b) for b in range(NT)]
+
+        def part(b):
+            return (b, 0) if b < 2 else (2, (b - 2) * QT)
+
+        nc.sync.dma_start(out=k_raw[0][:], in_=k_src[:, :, 0 : N // 2])
+        nc.sync.dma_start(out=k_raw[1][:], in_=k_src[:, :, N // 2 : N])
+        nc.sync.dma_start(out=q_raw[0][:], in_=q_src[:, :, 0:QT])
+        nc.sync.dma_start(out=t_sb[:], in_=t_src)
+        nc.sync.dma_start(out=mask_raw[0][:], in_=mask_src[:, :, 0:QT])
+        nc.sync.dma_start(out=q_raw[1][:], in_=q_src[:, :, QT : 2 * QT])
+        nc.sync.dma_start(out=q_raw[2][:], in_=q_src[:, :, 2 * QT : NQ])
+        nc.sync.dma_start(out=mask_raw[1][:], in_=mask_src[:, :, QT : 2 * QT])
+        nc.sync.dma_start(out=v_raw[0][:], in_=v_src[:, 0:2, :, :])
+        nc.sync.dma_start(out=mask_raw[2][:], in_=mask_src[:, :, 2 * QT : NQ])
+        nc.sync.dma_start(out=v_raw[1][:], in_=v_src[:, 2:4, :, :])
+        for b in range(NT):
+            nc.sync.dma_start(out=og_raw[b][:], in_=og_src[b])
+
+        def pack_k(h):
+            s = slice(h * (P // 2), (h + 1) * (P // 2))
+            nc.vector.tensor_copy(
+                out=k_bf[:, :, s, :].rearrange("p r s j -> p s j r"),
+                in_=k_raw[h][:].rearrange("p j (s r) -> p s j r", r=PACK),
+            )
+
+        def pack(copy, dst, src):
+            copy(
+                out=dst.rearrange("p (c i) j -> p c j i", i=4),
+                in_=src.rearrange("p j (c i) -> p c j i", i=4),
+            )
+
+        def quantize(codes, scales, src):
+            nc.vector.quantize_mx(out=codes.bitcast(FP8X4), scales=scales, in_=src)
+
+        def quantize_q(i):
+            quantize(q_codes[i][:], q_scales[i][:], q_bf[i][:].rearrange("p c j -> p (c j)"))
+
+        def quantize_v(i):
+            quantize(v_codes[i][:], v_scales[i][:], v_bf[i][:].rearrange("p g e r -> p (g e r)"))
+
+        def quantize_w(b, half):
+            i = 2 * b + half
+            quantize(w_codes[i][:], w_scales[i][:], w_bf[i][:].rearrange("p g x -> p (g x)"))
+
+        def pack_v(g):
+            pack(nc.scalar.copy, v_bf[g // 2][:, g % 2, :, :], v_raw[g // 2][:, g % 2, :, :])
+
+        def scores(b):
+            i, c0 = part(b)
+            for g in range(H):
+                rows = slice(ROWS * g, ROWS * (g + 1))
+                for r in range(PACK):
+                    cols = slice(P * r, P * (r + 1))
+                    nc.tensor.matmul_mx(
+                        out=score[g][:, r, :],
+                        lhsT=k_codes[rows, cols].bitcast(FP8X4),
+                        lhsT_scale=k_scales[rows, cols],
+                        rhs=q_codes[i][rows, c0 : c0 + QT].bitcast(FP8X4),
+                        rhs_scale=q_scales[i][rows, c0 : c0 + QT],
+                        start=True,
+                        stop=True,
+                    )
+
+        def values(b, heads):
+            for g in heads:
+                i = 2 * b + g // 2
+                wc = slice((g % 2) * QT, (g % 2 + 1) * QT)
+                vc = slice((g % 2) * D, (g % 2 + 1) * D)
+                nc.tensor.matmul_mx(
+                    out=y[b][:, g, :],
+                    lhsT=w_codes[i][:, wc].bitcast(FP8X4),
+                    lhsT_scale=w_scales[i][:, wc],
+                    rhs=v_codes[g // 2][:, vc].bitcast(FP8X4),
+                    rhs_scale=v_scales[g // 2][:, vc],
+                    start=True,
+                    stop=True,
+                )
+
+        def exp(b, g):
+            nc.scalar.activation(out=p_f[H * b + g][:], in_=score[g][:].rearrange("p r n -> p n r"), func=ACT.Exp)
+
+        def mask_times_t(b):
+            i, c0 = part(b)
+            nc.vector.tensor_tensor(
+                out=mt[b][:],
+                in0=mask_raw[i][:, :, c0 : c0 + QT].rearrange("p r n -> p n r"),
+                in1=t_sb[:].rearrange("p (a r) -> p a r", a=1).to_broadcast([P, QT, PACK]),
+                op=ALU.mult,
+            )
+
+        def weigh(b, g):
+            nc.vector.tensor_tensor(
+                out=w_bf[2 * b + g // 2][:, g % 2, :],
+                in0=p_f[H * b + g][:].rearrange("p n r -> p (n r)"),
+                in1=mt[b][:].rearrange("p n r -> p (n r)"),
+                op=ALU.mult,
+            )
+
+        def denominators(b):
+            nc.vector.reciprocal(out=rcp[b][:], in_=y[b][:, :, D - 1])
+
+        def finish(b):
+            for g in range(H):
+                nc.vector.scalar_tensor_tensor(
+                    out=res[b][:, g, :], in0=y[b][:, g, :], scalar=rcp[b][:, g : g + 1], in1=gate[b][:, g, :],
+                    op0=ALU.mult, op1=ALU.mult,
+                )
+            nc.sync.dma_start(out=out_dst[b], in_=res[b][:])
+
+        pack_k(0)
+        pack_k(1)
+        pack(nc.vector.tensor_copy, q_bf[0][:], q_raw[0][:])
+        quantize(k_codes[:], k_scales[:], k_bf[:].rearrange("p r s j -> p (r s j)"))
+        quantize_q(0)
+        scores(0)
+        mask_times_t(0)
+
+        exp(0, 0)
+        pack(nc.scalar.copy, q_bf[1][:], q_raw[1][:])
+        weigh(0, 0)
+        quantize_q(1)
+        for g in range(1, H):
+            exp(0, g)
+        scores(1)
+        weigh(0, 1)
+        mask_times_t(1)
+        weigh(0, 2)
+        quantize_w(0, 0)
+        weigh(0, 3)
+
+        exp(1, 0)
+        pack(nc.scalar.copy, q_bf[2][:], q_raw[2][:])
+        weigh(1, 0)
+        quantize_q(2)
+        for g in range(1, H):
+            exp(1, g)
+        scores(2)
+        quantize_w(0, 1)
+        weigh(1, 1)
+        mask_times_t(2)
+        weigh(1, 2)
+        quantize_w(1, 0)
+        weigh(1, 3)
+
+        exp(2, 0)
+        pack_v(0)
+        exp(2, 1)
+        pack_v(1)
+        exp(2, 2)
+        exp(2, 3)
+        scores(3)
+        weigh(2, 0)
+        quantize_w(1, 1)
+        weigh(2, 1)
+        quantize_v(0)
+        mask_times_t(3)
+        weigh(2, 2)
+        quantize_w(2, 0)
+        weigh(2, 3)
+
+        pack_v(2)
+        exp(3, 0)
+        pack_v(3)
+        for g in range(1, H):
+            exp(3, g)
+        for b in range(NT):
+            nc.scalar.activation(out=gate[b][:], in_=og_raw[b][:], func=ACT.Sigmoid)
+        weigh(3, 0)
+        quantize_w(2, 1)
+        quantize_v(1)
+        for b in range(3):
+            values(b, range(H))
+        weigh(3, 1)
+        weigh(3, 2)
+        quantize_w(3, 0)
+        values(3, range(2))
+        weigh(3, 3)
+        for b in range(3):
+            denominators(b)
+        quantize_w(3, 1)
+        values(3, range(2, H))
+        finish(0)
+        denominators(3)
+        for b in range(1, NT):
+            finish(b)

@@ -38,25 +38,25 @@ def tile_rows_mask_gate_kernel(tc, qT, kT, t, v, mask, og, out):
         def tiles(name, count, shape, dtype):
             return [sb.tile(shape, dtype, name="%s%d" % (name, i), align_bytes=64) for i in range(count)]
 
-        k_raw = tiles("k_raw", 2, [P, PACK, N // 2], F32)
+        k_raw = tiles("k_raw_first", 1, [P, PACK, N // 2], F32) + tiles("k_raw", 2, [P, PACK, N // 4], F32)
         q_raw = tiles("q_raw", 2, [P, PACK, QT], F32) + tiles("q_raw_late", 1, [P, PACK, 2 * QT], F32)
-        mask_raw = tiles("mask_raw", 2, [P, PACK, QT], F32) + tiles("mask_raw_late", 1, [P, PACK, 2 * QT], F32)
+        mask_raw = tiles("mask_raw", 2, [P, PACK, 2 * QT], F32)
         v_raw = tiles("v_raw", 2, [P, 2, PACK, D], F32)
         og_raw = tiles("og_raw", NT, [P, H, D], F32)
         t_sb = sb.tile([P, PACK], F32, name="t_sb", align_bytes=64)
 
-        k_bf = sb.tile([P, PACK, P, PACK], BF16, name="k_bf", align_bytes=64)
-        k_codes = sb.tile([P, N], U32, name="k_codes", align_bytes=64)
-        k_scales = sb.tile([P, N], U8, name="k_scales", align_bytes=64)
+        k_bf = tiles("k_bf", 2, [P, PACK, P // 2, PACK], BF16)
+        k_codes = tiles("k_codes", PACK, [P, P], U32)
+        k_scales = tiles("k_scales", PACK, [P, P], U8)
         q_bf = tiles("q_bf", 2, [P, QT, PACK], BF16) + tiles("q_bf_late", 1, [P, 2 * QT, PACK], BF16)
         q_codes = tiles("q_codes", 2, [P, QT], U32) + tiles("q_codes_late", 1, [P, 2 * QT], U32)
         q_scales = tiles("q_scales", 2, [P, QT], U8) + tiles("q_scales_late", 1, [P, 2 * QT], U8)
         v_bf = tiles("v_bf", 2, [P, 2, D, PACK], BF16)
         v_codes = tiles("v_codes", 2, [P, 2 * D], U32)
         v_scales = tiles("v_scales", 2, [P, 2 * D], U8)
-        mt = tiles("mt", NT, [P, QT, PACK], F32)
-        p_f = tiles("p_f", NT * H, [P, QT, PACK], F32)
-        w_bf = tiles("w_bf", NT * 2, [P, 2, QT * PACK], BF16)
+        mt = tiles("mt", 2, [P, PACK, 2 * QT], F32)
+        p_f = tiles("p_f", NT * H, [P, PACK, QT], F32)
+        w_bf = tiles("w_bf", NT * 2, [P, 2, QT, PACK], BF16)
         w_codes = tiles("w_codes", NT * 2, [P, 2 * QT], U32)
         w_scales = tiles("w_scales", NT * 2, [P, 2 * QT], U8)
         gate = tiles("gate", NT, [P, H, D], F32)
@@ -70,24 +70,24 @@ def tile_rows_mask_gate_kernel(tc, qT, kT, t, v, mask, og, out):
             return (b, 0) if b < 2 else (2, (b - 2) * QT)
 
         nc.sync.dma_start(out=k_raw[0][:], in_=k_src[:, :, 0 : N // 2])
-        nc.sync.dma_start(out=k_raw[1][:], in_=k_src[:, :, N // 2 : N])
+        nc.sync.dma_start(out=k_raw[1][:], in_=k_src[:, :, N // 2 : 3 * N // 4])
         nc.sync.dma_start(out=q_raw[0][:], in_=q_src[:, :, 0:QT])
+        nc.sync.dma_start(out=k_raw[2][:], in_=k_src[:, :, 3 * N // 4 : N])
         nc.sync.dma_start(out=t_sb[:], in_=t_src)
-        nc.sync.dma_start(out=mask_raw[0][:], in_=mask_src[:, :, 0:QT])
+        nc.sync.dma_start(out=mask_raw[0][:], in_=mask_src[:, :, 0 : 2 * QT])
         nc.sync.dma_start(out=q_raw[1][:], in_=q_src[:, :, QT : 2 * QT])
         nc.sync.dma_start(out=q_raw[2][:], in_=q_src[:, :, 2 * QT : NQ])
-        nc.sync.dma_start(out=mask_raw[1][:], in_=mask_src[:, :, QT : 2 * QT])
+        nc.sync.dma_start(out=mask_raw[1][:], in_=mask_src[:, :, 2 * QT : NQ])
         nc.sync.dma_start(out=v_raw[0][:], in_=v_src[:, 0:2, :, :])
-        nc.sync.dma_start(out=mask_raw[2][:], in_=mask_src[:, :, 2 * QT : NQ])
         nc.sync.dma_start(out=v_raw[1][:], in_=v_src[:, 2:4, :, :])
         for b in range(NT):
             nc.sync.dma_start(out=og_raw[b][:], in_=og_src[b])
 
-        def pack_k(h):
-            s = slice(h * (P // 2), (h + 1) * (P // 2))
+        def pack_k(i):
+            dst = k_bf[0][:] if i == 0 else k_bf[1][:, :, (i - 1) * (P // 4) : i * (P // 4), :]
             nc.vector.tensor_copy(
-                out=k_bf[:, :, s, :].rearrange("p r s j -> p s j r"),
-                in_=k_raw[h][:].rearrange("p j (s r) -> p s j r", r=PACK),
+                out=dst.rearrange("p r s j -> p s j r"),
+                in_=k_raw[i][:].rearrange("p j (s r) -> p s j r", r=PACK),
             )
 
         def pack(copy, dst, src):
@@ -99,6 +99,11 @@ def tile_rows_mask_gate_kernel(tc, qT, kT, t, v, mask, og, out):
         def quantize(codes, scales, src):
             nc.vector.quantize_mx(out=codes.bitcast(FP8X4), scales=scales, in_=src)
 
+        def quantize_k(h):
+            s = slice(h * (P // 2), (h + 1) * (P // 2))
+            for r in range(PACK):
+                quantize(k_codes[r][:, s], k_scales[r][:, s], k_bf[h][:, r, :, :].rearrange("p s j -> p (s j)"))
+
         def quantize_q(i):
             quantize(q_codes[i][:], q_scales[i][:], q_bf[i][:].rearrange("p c j -> p (c j)"))
 
@@ -107,26 +112,27 @@ def tile_rows_mask_gate_kernel(tc, qT, kT, t, v, mask, og, out):
 
         def quantize_w(b, half):
             i = 2 * b + half
-            quantize(w_codes[i][:], w_scales[i][:], w_bf[i][:].rearrange("p g x -> p (g x)"))
+            quantize(w_codes[i][:], w_scales[i][:], w_bf[i][:].rearrange("p g n r -> p (g n r)"))
 
-        def pack_v(g):
-            pack(nc.scalar.copy, v_bf[g // 2][:, g % 2, :, :], v_raw[g // 2][:, g % 2, :, :])
+        def pack_v(copy, g):
+            pack(copy, v_bf[g // 2][:, g % 2, :, :], v_raw[g // 2][:, g % 2, :, :])
 
-        def scores(b):
+        def scores(b, order):
             i, c0 = part(b)
-            for g in range(H):
+            for g, r in order:
                 rows = slice(ROWS * g, ROWS * (g + 1))
-                for r in range(PACK):
-                    cols = slice(P * r, P * (r + 1))
-                    nc.tensor.matmul_mx(
-                        out=score[g][:, r, :],
-                        lhsT=k_codes[rows, cols].bitcast(FP8X4),
-                        lhsT_scale=k_scales[rows, cols],
-                        rhs=q_codes[i][rows, c0 : c0 + QT].bitcast(FP8X4),
-                        rhs_scale=q_scales[i][rows, c0 : c0 + QT],
-                        start=True,
-                        stop=True,
-                    )
+                nc.tensor.matmul_mx(
+                    out=score[g][:, r, :],
+                    lhsT=k_codes[r][rows, :].bitcast(FP8X4),
+                    lhsT_scale=k_scales[r][rows, :],
+                    rhs=q_codes[i][rows, c0 : c0 + QT].bitcast(FP8X4),
+                    rhs_scale=q_scales[i][rows, c0 : c0 + QT],
+                    start=True,
+                    stop=True,
+                )
+
+        by_slot = [(g, r) for r in range(PACK) for g in range(H)]
+        by_head = [(g, r) for g in range(H) for r in range(PACK)]
 
         def values(b, heads):
             for g in heads:
@@ -144,22 +150,20 @@ def tile_rows_mask_gate_kernel(tc, qT, kT, t, v, mask, og, out):
                 )
 
         def exp(b, g):
-            nc.scalar.activation(out=p_f[H * b + g][:], in_=score[g][:].rearrange("p r n -> p n r"), func=ACT.Exp)
+            nc.scalar.activation(out=p_f[H * b + g][:], in_=score[g][:], func=ACT.Exp)
 
-        def mask_times_t(b):
-            i, c0 = part(b)
-            nc.vector.tensor_tensor(
-                out=mt[b][:],
-                in0=mask_raw[i][:, :, c0 : c0 + QT].rearrange("p r n -> p n r"),
-                in1=t_sb[:].rearrange("p (a r) -> p a r", a=1).to_broadcast([P, QT, PACK]),
-                op=ALU.mult,
-            )
+        def mask_times_t(h):
+            for r in range(PACK):
+                nc.vector.tensor_scalar(
+                    out=mt[h][:, r, :], in0=mask_raw[h][:, r, :], scalar1=t_sb[:, r : r + 1], scalar2=None, op0=ALU.mult
+                )
 
         def weigh(b, g):
+            c0 = (b % 2) * QT
             nc.vector.tensor_tensor(
-                out=w_bf[2 * b + g // 2][:, g % 2, :],
-                in0=p_f[H * b + g][:].rearrange("p n r -> p (n r)"),
-                in1=mt[b][:].rearrange("p n r -> p (n r)"),
+                out=w_bf[2 * b + g // 2][:, g % 2, :, :].rearrange("p (c i) r -> p c r i", i=2),
+                in0=p_f[H * b + g][:].rearrange("p r (c i) -> p c r i", i=2),
+                in1=mt[b // 2][:, :, c0 : c0 + QT].rearrange("p r (c i) -> p c r i", i=2),
                 op=ALU.mult,
             )
 
@@ -176,21 +180,22 @@ def tile_rows_mask_gate_kernel(tc, qT, kT, t, v, mask, og, out):
 
         pack_k(0)
         pack_k(1)
+        quantize_k(0)
         pack(nc.vector.tensor_copy, q_bf[0][:], q_raw[0][:])
-        quantize(k_codes[:], k_scales[:], k_bf[:].rearrange("p r s j -> p (r s j)"))
+        pack_k(2)
         quantize_q(0)
-        scores(0)
+        quantize_k(1)
+        scores(0, by_slot)
         mask_times_t(0)
+        pack(nc.vector.tensor_copy, q_bf[1][:], q_raw[1][:])
 
         exp(0, 0)
-        pack(nc.scalar.copy, q_bf[1][:], q_raw[1][:])
         weigh(0, 0)
         quantize_q(1)
         for g in range(1, H):
             exp(0, g)
-        scores(1)
+        scores(1, by_head)
         weigh(0, 1)
-        mask_times_t(1)
         weigh(0, 2)
         quantize_w(0, 0)
         weigh(0, 3)
@@ -198,43 +203,41 @@ def tile_rows_mask_gate_kernel(tc, qT, kT, t, v, mask, og, out):
         exp(1, 0)
         pack(nc.scalar.copy, q_bf[2][:], q_raw[2][:])
         weigh(1, 0)
+        quantize_w(0, 1)
+        mask_times_t(1)
         quantize_q(2)
         for g in range(1, H):
             exp(1, g)
-        scores(2)
-        quantize_w(0, 1)
+        scores(2, by_head)
         weigh(1, 1)
-        mask_times_t(2)
         weigh(1, 2)
         quantize_w(1, 0)
         weigh(1, 3)
 
         exp(2, 0)
-        pack_v(0)
+        pack_v(nc.scalar.copy, 0)
         exp(2, 1)
-        pack_v(1)
+        pack_v(nc.scalar.copy, 1)
         exp(2, 2)
         exp(2, 3)
-        scores(3)
+        scores(3, by_head)
         weigh(2, 0)
         quantize_w(1, 1)
+        pack_v(nc.vector.tensor_copy, 2)
         weigh(2, 1)
         quantize_v(0)
-        mask_times_t(3)
         weigh(2, 2)
         quantize_w(2, 0)
         weigh(2, 3)
 
-        pack_v(2)
-        exp(3, 0)
-        pack_v(3)
-        for g in range(1, H):
+        pack_v(nc.scalar.copy, 3)
+        for g in range(H):
             exp(3, g)
         for b in range(NT):
             nc.scalar.activation(out=gate[b][:], in_=og_raw[b][:], func=ACT.Sigmoid)
+        quantize_v(1)
         weigh(3, 0)
         quantize_w(2, 1)
-        quantize_v(1)
         for b in range(3):
             values(b, range(H))
         weigh(3, 1)

@@ -38,14 +38,14 @@ def tile_rows_mask_gate_kernel(tc, qT, kT, t, v, mask, og, out):
         def tiles(name, count, shape, dtype):
             return [sb.tile(shape, dtype, name="%s%d" % (name, i), align_bytes=64) for i in range(count)]
 
-        k_raw = tiles("k_raw_first", 1, [P, PACK, N // 2], F32) + tiles("k_raw", 2, [P, PACK, N // 4], F32)
+        k_raw = tiles("k_raw", 2, [P, 2, N], F32)
         q_raw = tiles("q_raw", 2, [P, PACK, QT], F32) + tiles("q_raw_late", 1, [P, PACK, 2 * QT], F32)
-        mask_raw = tiles("mask_raw", 2, [P, PACK, 2 * QT], F32)
+        mask_raw = tiles("mask_raw", 1, [P, PACK, QT], F32) + tiles("mask_raw_late", 1, [P, PACK, 3 * QT], F32)
         v_raw = tiles("v_raw", 2, [P, 2, PACK, D], F32)
         og_raw = tiles("og_raw", NT, [P, H, D], F32)
         t_sb = sb.tile([P, PACK], F32, name="t_sb", align_bytes=64)
 
-        k_bf = tiles("k_bf", 2, [P, PACK, P // 2, PACK], BF16)
+        k_bf = sb.tile([P, PACK, P, PACK], BF16, name="k_bf", align_bytes=64)
         k_codes = tiles("k_codes", PACK, [P, P], U32)
         k_scales = tiles("k_scales", PACK, [P, P], U8)
         q_bf = tiles("q_bf", 2, [P, QT, PACK], BF16) + tiles("q_bf_late", 1, [P, 2 * QT, PACK], BF16)
@@ -54,7 +54,7 @@ def tile_rows_mask_gate_kernel(tc, qT, kT, t, v, mask, og, out):
         v_bf = tiles("v_bf", 2, [P, 2, D, PACK], BF16)
         v_codes = tiles("v_codes", 2, [P, 2 * D], U32)
         v_scales = tiles("v_scales", 2, [P, 2 * D], U8)
-        mt = tiles("mt", 2, [P, PACK, 2 * QT], F32)
+        mt = tiles("mt", 1, [P, PACK, QT], F32) + tiles("mt_late", 1, [P, PACK, 3 * QT], F32)
         p_f = tiles("p_f", NT * H, [P, PACK, QT], F32)
         w_bf = tiles("w_bf", NT * 2, [P, 2, QT, PACK], BF16)
         w_codes = tiles("w_codes", NT * 2, [P, 2 * QT], U32)
@@ -69,25 +69,23 @@ def tile_rows_mask_gate_kernel(tc, qT, kT, t, v, mask, og, out):
         def part(b):
             return (b, 0) if b < 2 else (2, (b - 2) * QT)
 
-        nc.sync.dma_start(out=k_raw[0][:], in_=k_src[:, :, 0 : N // 2])
-        nc.sync.dma_start(out=k_raw[1][:], in_=k_src[:, :, N // 2 : 3 * N // 4])
+        nc.scalar.dma_start(out=t_sb[:], in_=t_src)
+        nc.sync.dma_start(out=k_raw[0][:], in_=k_src[:, 0:2, :])
+        nc.sync.dma_start(out=k_raw[1][:], in_=k_src[:, 2:4, :])
         nc.sync.dma_start(out=q_raw[0][:], in_=q_src[:, :, 0:QT])
-        nc.sync.dma_start(out=k_raw[2][:], in_=k_src[:, :, 3 * N // 4 : N])
-        nc.sync.dma_start(out=t_sb[:], in_=t_src)
-        nc.sync.dma_start(out=mask_raw[0][:], in_=mask_src[:, :, 0 : 2 * QT])
+        nc.sync.dma_start(out=mask_raw[0][:], in_=mask_src[:, :, 0:QT])
         nc.sync.dma_start(out=q_raw[1][:], in_=q_src[:, :, QT : 2 * QT])
+        nc.sync.dma_start(out=mask_raw[1][:], in_=mask_src[:, :, QT:NQ])
         nc.sync.dma_start(out=q_raw[2][:], in_=q_src[:, :, 2 * QT : NQ])
-        nc.sync.dma_start(out=mask_raw[1][:], in_=mask_src[:, :, 2 * QT : NQ])
         nc.sync.dma_start(out=v_raw[0][:], in_=v_src[:, 0:2, :, :])
         nc.sync.dma_start(out=v_raw[1][:], in_=v_src[:, 2:4, :, :])
         for b in range(NT):
             nc.sync.dma_start(out=og_raw[b][:], in_=og_src[b])
 
-        def pack_k(i):
-            dst = k_bf[0][:] if i == 0 else k_bf[1][:, :, (i - 1) * (P // 4) : i * (P // 4), :]
+        def pack_k(h):
             nc.vector.tensor_copy(
-                out=dst.rearrange("p r s j -> p s j r"),
-                in_=k_raw[i][:].rearrange("p j (s r) -> p s j r", r=PACK),
+                out=k_bf[:, :, :, 2 * h : 2 * h + 2].rearrange("p r s j -> p s j r"),
+                in_=k_raw[h][:].rearrange("p j (s r) -> p s j r", r=PACK),
             )
 
         def pack(copy, dst, src):
@@ -99,10 +97,8 @@ def tile_rows_mask_gate_kernel(tc, qT, kT, t, v, mask, og, out):
         def quantize(codes, scales, src):
             nc.vector.quantize_mx(out=codes.bitcast(FP8X4), scales=scales, in_=src)
 
-        def quantize_k(h):
-            s = slice(h * (P // 2), (h + 1) * (P // 2))
-            for r in range(PACK):
-                quantize(k_codes[r][:, s], k_scales[r][:, s], k_bf[h][:, r, :, :].rearrange("p s j -> p (s j)"))
+        def quantize_k(r):
+            quantize(k_codes[r][:], k_scales[r][:], k_bf[:, r, :, :].rearrange("p s j -> p (s j)"))
 
         def quantize_q(i):
             quantize(q_codes[i][:], q_scales[i][:], q_bf[i][:].rearrange("p c j -> p (c j)"))
@@ -131,7 +127,7 @@ def tile_rows_mask_gate_kernel(tc, qT, kT, t, v, mask, og, out):
                     stop=True,
                 )
 
-        by_slot = [(g, r) for r in range(PACK) for g in range(H)]
+        by_pair = [(g0 + g, r) for g0 in (0, 2) for r in range(PACK) for g in range(2)]
         by_head = [(g, r) for g in range(H) for r in range(PACK)]
 
         def values(b, heads):
@@ -159,33 +155,34 @@ def tile_rows_mask_gate_kernel(tc, qT, kT, t, v, mask, og, out):
                 )
 
         def weigh(b, g):
-            c0 = (b % 2) * QT
+            m, c0 = (0, 0) if b == 0 else (1, (b - 1) * QT)
             nc.vector.tensor_tensor(
                 out=w_bf[2 * b + g // 2][:, g % 2, :, :].rearrange("p (c i) r -> p c r i", i=2),
                 in0=p_f[H * b + g][:].rearrange("p r (c i) -> p c r i", i=2),
-                in1=mt[b // 2][:, :, c0 : c0 + QT].rearrange("p r (c i) -> p c r i", i=2),
+                in1=mt[m][:, :, c0 : c0 + QT].rearrange("p r (c i) -> p c r i", i=2),
                 op=ALU.mult,
             )
 
         def denominators(b):
             nc.vector.reciprocal(out=rcp[b][:], in_=y[b][:, :, D - 1])
 
-        def finish(b):
-            for g in range(H):
+        def finish(b, heads):
+            for g in heads:
                 nc.vector.scalar_tensor_tensor(
                     out=res[b][:, g, :], in0=y[b][:, g, :], scalar=rcp[b][:, g : g + 1], in1=gate[b][:, g, :],
                     op0=ALU.mult, op1=ALU.mult,
                 )
-            nc.sync.dma_start(out=out_dst[b], in_=res[b][:])
+            hs = slice(heads.start, heads.stop)
+            nc.sync.dma_start(out=out_dst[b][:, hs, :], in_=res[b][:, hs, :])
 
         pack_k(0)
         pack_k(1)
-        quantize_k(0)
         pack(nc.vector.tensor_copy, q_bf[0][:], q_raw[0][:])
-        pack_k(2)
+        quantize_k(0)
         quantize_q(0)
-        quantize_k(1)
-        scores(0, by_slot)
+        for r in range(1, PACK):
+            quantize_k(r)
+        scores(0, by_pair)
         mask_times_t(0)
         pack(nc.vector.tensor_copy, q_bf[1][:], q_raw[1][:])
 
@@ -198,18 +195,19 @@ def tile_rows_mask_gate_kernel(tc, qT, kT, t, v, mask, og, out):
         weigh(0, 1)
         weigh(0, 2)
         quantize_w(0, 0)
+        mask_times_t(1)
         weigh(0, 3)
 
         exp(1, 0)
+        exp(1, 1)
         pack(nc.scalar.copy, q_bf[2][:], q_raw[2][:])
         weigh(1, 0)
         quantize_w(0, 1)
-        mask_times_t(1)
-        quantize_q(2)
-        for g in range(1, H):
-            exp(1, g)
-        scores(2, by_head)
         weigh(1, 1)
+        quantize_q(2)
+        exp(1, 2)
+        exp(1, 3)
+        scores(2, by_head)
         weigh(1, 2)
         quantize_w(1, 0)
         weigh(1, 3)
@@ -249,7 +247,9 @@ def tile_rows_mask_gate_kernel(tc, qT, kT, t, v, mask, og, out):
             denominators(b)
         quantize_w(3, 1)
         values(3, range(2, H))
-        finish(0)
+        finish(0, range(0, 2))
         denominators(3)
+        finish(0, range(2, H))
         for b in range(1, NT):
-            finish(b)
+            finish(b, range(0, 2))
+            finish(b, range(2, H))

@@ -40,7 +40,7 @@ def tile_rows_mask_gate_kernel(tc, qT, kT, t, v, mask, og, out):
 
         k_raw = tiles("k_raw", 2, [P, 2, N], F32)
         q_raw = tiles("q_raw", 2, [P, PACK, QT], F32) + tiles("q_raw_late", 1, [P, PACK, 2 * QT], F32)
-        mask_raw = tiles("mask_raw", 1, [P, PACK, QT], F32) + tiles("mask_raw_late", 1, [P, PACK, 3 * QT], F32)
+        mask_raw = tiles("mask_raw", 2, [P, PACK, QT], F32) + tiles("mask_raw_late", 1, [P, PACK, 2 * QT], F32)
         v_raw = tiles("v_raw", 2, [P, 2, PACK, D], F32)
         og_raw = tiles("og_raw", NT, [P, H, D], F32)
         t_sb = sb.tile([P, PACK], F32, name="t_sb", align_bytes=64)
@@ -54,7 +54,7 @@ def tile_rows_mask_gate_kernel(tc, qT, kT, t, v, mask, og, out):
         v_bf = tiles("v_bf", 2, [P, 2, D, PACK], BF16)
         v_codes = tiles("v_codes", 2, [P, 2 * D], U32)
         v_scales = tiles("v_scales", 2, [P, 2 * D], U8)
-        mt = tiles("mt", 1, [P, PACK, QT], F32) + tiles("mt_late", 1, [P, PACK, 3 * QT], F32)
+        mt = tiles("mt", 2, [P, PACK, QT], F32) + tiles("mt_late", 1, [P, PACK, 2 * QT], F32)
         p_f = tiles("p_f", NT * H, [P, PACK, QT], F32)
         w_bf = tiles("w_bf", NT * 2, [P, 2, QT, PACK], BF16)
         w_codes = tiles("w_codes", NT * 2, [P, 2 * QT], U32)
@@ -69,14 +69,15 @@ def tile_rows_mask_gate_kernel(tc, qT, kT, t, v, mask, og, out):
         def part(b):
             return (b, 0) if b < 2 else (2, (b - 2) * QT)
 
-        nc.scalar.dma_start(out=t_sb[:], in_=t_src)
         nc.sync.dma_start(out=k_raw[0][:], in_=k_src[:, 0:2, :])
         nc.sync.dma_start(out=k_raw[1][:], in_=k_src[:, 2:4, :])
         nc.sync.dma_start(out=q_raw[0][:], in_=q_src[:, :, 0:QT])
-        nc.sync.dma_start(out=mask_raw[0][:], in_=mask_src[:, :, 0:QT])
         nc.sync.dma_start(out=q_raw[1][:], in_=q_src[:, :, QT : 2 * QT])
-        nc.sync.dma_start(out=mask_raw[1][:], in_=mask_src[:, :, QT:NQ])
+        nc.sync.dma_start(out=t_sb[:], in_=t_src)
+        nc.sync.dma_start(out=mask_raw[0][:], in_=mask_src[:, :, 0:QT])
+        nc.sync.dma_start(out=mask_raw[1][:], in_=mask_src[:, :, QT : 2 * QT])
         nc.sync.dma_start(out=q_raw[2][:], in_=q_src[:, :, 2 * QT : NQ])
+        nc.sync.dma_start(out=mask_raw[2][:], in_=mask_src[:, :, 2 * QT : NQ])
         nc.sync.dma_start(out=v_raw[0][:], in_=v_src[:, 0:2, :, :])
         nc.sync.dma_start(out=v_raw[1][:], in_=v_src[:, 2:4, :, :])
         for b in range(NT):
@@ -155,7 +156,7 @@ def tile_rows_mask_gate_kernel(tc, qT, kT, t, v, mask, og, out):
                 )
 
         def weigh(b, g):
-            m, c0 = (0, 0) if b == 0 else (1, (b - 1) * QT)
+            m, c0 = part(b)
             nc.vector.tensor_tensor(
                 out=w_bf[2 * b + g // 2][:, g % 2, :, :].rearrange("p (c i) r -> p c r i", i=2),
                 in0=p_f[H * b + g][:].rearrange("p r (c i) -> p c r i", i=2),
@@ -183,12 +184,12 @@ def tile_rows_mask_gate_kernel(tc, qT, kT, t, v, mask, og, out):
         for r in range(1, PACK):
             quantize_k(r)
         scores(0, by_pair)
-        mask_times_t(0)
         pack(nc.vector.tensor_copy, q_bf[1][:], q_raw[1][:])
+        quantize_q(1)
+        mask_times_t(0)
 
         exp(0, 0)
         weigh(0, 0)
-        quantize_q(1)
         for g in range(1, H):
             exp(0, g)
         scores(1, by_head)
@@ -199,17 +200,17 @@ def tile_rows_mask_gate_kernel(tc, qT, kT, t, v, mask, og, out):
         weigh(0, 3)
 
         exp(1, 0)
-        exp(1, 1)
         pack(nc.scalar.copy, q_bf[2][:], q_raw[2][:])
         weigh(1, 0)
         quantize_w(0, 1)
-        weigh(1, 1)
         quantize_q(2)
-        exp(1, 2)
-        exp(1, 3)
+        for g in range(1, H):
+            exp(1, g)
         scores(2, by_head)
+        weigh(1, 1)
         weigh(1, 2)
         quantize_w(1, 0)
+        mask_times_t(2)
         weigh(1, 3)
 
         exp(2, 0)
@@ -232,7 +233,11 @@ def tile_rows_mask_gate_kernel(tc, qT, kT, t, v, mask, og, out):
         for g in range(H):
             exp(3, g)
         for b in range(NT):
-            nc.scalar.activation(out=gate[b][:], in_=og_raw[b][:], func=ACT.Sigmoid)
+            step = 2 if b in (0, NT - 1) else H
+            for g0 in range(0, H, step):
+                nc.scalar.activation(
+                    out=gate[b][:, g0 : g0 + step, :], in_=og_raw[b][:, g0 : g0 + step, :], func=ACT.Sigmoid
+                )
         quantize_v(1)
         weigh(3, 0)
         quantize_w(2, 1)
@@ -247,9 +252,9 @@ def tile_rows_mask_gate_kernel(tc, qT, kT, t, v, mask, og, out):
             denominators(b)
         quantize_w(3, 1)
         values(3, range(2, H))
-        finish(0, range(0, 2))
+        finish(0, range(H))
+        finish(1, range(H))
         denominators(3)
-        finish(0, range(2, H))
-        for b in range(1, NT):
-            finish(b, range(0, 2))
-            finish(b, range(2, H))
+        finish(2, range(H))
+        finish(3, range(0, 2))
+        finish(3, range(2, H))

from contextlib import ExitStack

import concourse.mybir as mybir

H, D, NQ, N = 4, 128, 512, 512
FLOPS = 2 * 2 * H * NQ * N * D

F32 = mybir.dt.float32
BF16 = mybir.dt.bfloat16
U32 = mybir.dt.uint32
U8 = mybir.dt.uint8
FP8X4 = mybir.dt.float8_e4m3fn_x4
ACT = mybir.ActivationFunctionType
ALU = mybir.AluOpType

P = 128
PACK = 4
ROWS = 32
QT = 128
NT = NQ // QT


def tile_rows_mask_gate_kernel(tc, qT, kT, t, v, mask, og, out):
    nc = tc.nc
    q_src = qT.rearrange("g (p j) c -> (g p) j c", j=PACK)
    k_src = kT.rearrange("g (p j) c -> (g p) j c", j=PACK)
    v_src = v.rearrange("g (p r) e -> p g r e", r=PACK)
    t_src = t.rearrange("(p r) o -> p (r o)", r=PACK)
    mask_src = mask.rearrange("(p r) c -> p r c", r=PACK)
    og_src = og.rearrange("g (b p) e -> b p g e", p=QT)
    out_dst = out.rearrange("g (b p) e -> b p g e", p=QT)

    with ExitStack() as ctx:
        sb = ctx.enter_context(tc.tile_pool(name="sb", bufs=1))
        ps = ctx.enter_context(tc.psum_pool(name="ps", bufs=1))
        ctx.enter_context(tc.manual_schedule())

        def tiles(name, count, shape, dtype):
            return [sb.tile(shape, dtype, name="%s%d" % (name, i), align_bytes=64) for i in range(count)]

        k_raw = tiles("k_raw", 2, [P, 2, N], F32)
        q_raw = tiles("q_raw", 2, [P, PACK, QT], F32) + tiles("q_raw_late", 1, [P, PACK, 2 * QT], F32)
        mask_raw = tiles("mask_raw", 2, [P, PACK, QT], F32) + tiles("mask_raw_late", 1, [P, PACK, 2 * QT], F32)
        v_raw = tiles("v_raw", 2, [P, 2, PACK, D], F32)
        og_raw = tiles("og_raw", NT, [P, H, D], F32)
        t_sb = sb.tile([P, PACK], F32, name="t_sb", align_bytes=64)

        k_bf = sb.tile([P, PACK, P, PACK], BF16, name="k_bf", align_bytes=64)
        k_codes = tiles("k_codes", PACK, [P, P], U32)
        k_scales = tiles("k_scales", PACK, [P, P], U8)
        q_bf = tiles("q_bf", 2, [P, QT, PACK], BF16) + tiles("q_bf_late", 1, [P, 2 * QT, PACK], BF16)
        q_codes = tiles("q_codes", 2, [P, QT], U32) + tiles("q_codes_late", 1, [P, 2 * QT], U32)
        q_scales = tiles("q_scales", 2, [P, QT], U8) + tiles("q_scales_late", 1, [P, 2 * QT], U8)
        v_bf = tiles("v_bf", 2, [P, 2, D, PACK], BF16)
        v_codes = tiles("v_codes", 2, [P, 2 * D], U32)
        v_scales = tiles("v_scales", 2, [P, 2 * D], U8)
        mt = tiles("mt", 2, [P, PACK, QT], F32) + tiles("mt_late", 1, [P, PACK, 2 * QT], F32)
        p_f = tiles("p_f", NT * H, [P, PACK, QT], F32)
        w_bf = tiles("w_bf", NT * 2, [P, 2, QT, PACK], BF16)
        w_codes = tiles("w_codes", NT * 2, [P, 2 * QT], U32)
        w_scales = tiles("w_scales", NT * 2, [P, 2 * QT], U8)
        gate = tiles("gate", NT, [P, H, D], F32)
        rcp = tiles("rcp", NT, [P, H], F32)
        res = tiles("res", NT, [P, H, D], F32)

        score = [ps.tile([P, PACK, QT], F32, name="score%d" % g) for g in range(H)]
        y = [ps.tile([P, H, D], F32, name="y%d" % b) for b in range(NT)]

        def part(b):
            return (b, 0) if b < 2 else (2, (b - 2) * QT)

        nc.sync.dma_start(out=k_raw[0][:], in_=k_src[:, 0:2, :])
        nc.sync.dma_start(out=k_raw[1][:], in_=k_src[:, 2:4, :])
        nc.sync.dma_start(out=q_raw[0][:], in_=q_src[:, :, 0:QT])
        nc.sync.dma_start(out=q_raw[1][:], in_=q_src[:, :, QT : 2 * QT])
        nc.sync.dma_start(out=t_sb[:], in_=t_src)
        nc.sync.dma_start(out=mask_raw[0][:], in_=mask_src[:, :, 0:QT])
        nc.sync.dma_start(out=mask_raw[1][:], in_=mask_src[:, :, QT : 2 * QT])
        nc.sync.dma_start(out=q_raw[2][:], in_=q_src[:, :, 2 * QT : NQ])
        nc.sync.dma_start(out=mask_raw[2][:], in_=mask_src[:, :, 2 * QT : NQ])
        nc.sync.dma_start(out=v_raw[0][:], in_=v_src[:, 0:2, :, :])
        nc.sync.dma_start(out=v_raw[1][:], in_=v_src[:, 2:4, :, :])
        for b in range(NT):
            nc.sync.dma_start(out=og_raw[b][:], in_=og_src[b])

        def pack_k(h):
            nc.vector.tensor_copy(
                out=k_bf[:, :, :, 2 * h : 2 * h + 2].rearrange("p r s j -> p s j r"),
                in_=k_raw[h][:].rearrange("p j (s r) -> p s j r", r=PACK),
            )

        def pack(copy, dst, src):
            copy(
                out=dst.rearrange("p (c i) j -> p c j i", i=4),
                in_=src.rearrange("p j (c i) -> p c j i", i=4),
            )

        def quantize(codes, scales, src):
            nc.vector.quantize_mx(out=codes.bitcast(FP8X4), scales=scales, in_=src)

        def quantize_k(r):
            quantize(k_codes[r][:], k_scales[r][:], k_bf[:, r, :, :].rearrange("p s j -> p (s j)"))

        def quantize_q(i):
            quantize(q_codes[i][:], q_scales[i][:], q_bf[i][:].rearrange("p c j -> p (c j)"))

        def quantize_v(i):
            quantize(v_codes[i][:], v_scales[i][:], v_bf[i][:].rearrange("p g e r -> p (g e r)"))

        def quantize_w(b, half):
            i = 2 * b + half
            quantize(w_codes[i][:], w_scales[i][:], w_bf[i][:].rearrange("p g n r -> p (g n r)"))

        def pack_v(copy, g):
            pack(copy, v_bf[g // 2][:, g % 2, :, :], v_raw[g // 2][:, g % 2, :, :])

        def scores(b, order):
            i, c0 = part(b)
            for g, r in order:
                rows = slice(ROWS * g, ROWS * (g + 1))
                nc.tensor.matmul_mx(
                    out=score[g][:, r, :],
                    lhsT=k_codes[r][rows, :].bitcast(FP8X4),
                    lhsT_scale=k_scales[r][rows, :],
                    rhs=q_codes[i][rows, c0 : c0 + QT].bitcast(FP8X4),
                    rhs_scale=q_scales[i][rows, c0 : c0 + QT],
                    start=True,
                    stop=True,
                )

        by_pair = [(g0 + g, r) for g0 in (0, 2) for r in range(PACK) for g in range(2)]
        by_head = [(g, r) for g in range(H) for r in range(PACK)]

        def values(b, heads):
            for g in heads:
                i = 2 * b + g // 2
                wc = slice((g % 2) * QT, (g % 2 + 1) * QT)
                vc = slice((g % 2) * D, (g % 2 + 1) * D)
                nc.tensor.matmul_mx(
                    out=y[b][:, g, :],
                    lhsT=w_codes[i][:, wc].bitcast(FP8X4),
                    lhsT_scale=w_scales[i][:, wc],
                    rhs=v_codes[g // 2][:, vc].bitcast(FP8X4),
                    rhs_scale=v_scales[g // 2][:, vc],
                    start=True,
                    stop=True,
                )

        def exp(b, g):
            nc.scalar.activation(out=p_f[H * b + g][:], in_=score[g][:], func=ACT.Exp)

        def mask_times_t(h):
            for r in range(PACK):
                nc.vector.tensor_scalar(
                    out=mt[h][:, r, :], in0=mask_raw[h][:, r, :], scalar1=t_sb[:, r : r + 1], scalar2=None, op0=ALU.mult
                )

        def weigh(b, g):
            m, c0 = part(b)
            nc.vector.tensor_tensor(
                out=w_bf[2 * b + g // 2][:, g % 2, :, :].rearrange("p (c i) r -> p c r i", i=2),
                in0=p_f[H * b + g][:].rearrange("p r (c i) -> p c r i", i=2),
                in1=mt[m][:, :, c0 : c0 + QT].rearrange("p r (c i) -> p c r i", i=2),
                op=ALU.mult,
            )

        def denominators(b):
            nc.vector.reciprocal(out=rcp[b][:], in_=y[b][:, :, D - 1])

        def finish(b, heads):
            for g in heads:
                nc.vector.scalar_tensor_tensor(
                    out=res[b][:, g, :], in0=y[b][:, g, :], scalar=rcp[b][:, g : g + 1], in1=gate[b][:, g, :],
                    op0=ALU.mult, op1=ALU.mult,
                )
            hs = slice(heads.start, heads.stop)
            nc.sync.dma_start(out=out_dst[b][:, hs, :], in_=res[b][:, hs, :])

        pack_k(0)
        pack_k(1)
        pack(nc.vector.tensor_copy, q_bf[0][:], q_raw[0][:])
        quantize_k(0)
        quantize_q(0)
        for r in range(1, PACK):
            quantize_k(r)
        scores(0, by_pair)
        pack(nc.vector.tensor_copy, q_bf[1][:], q_raw[1][:])
        quantize_q(1)
        mask_times_t(0)

        exp(0, 0)
        weigh(0, 0)
        for g in range(1, H):
            exp(0, g)
        scores(1, by_head)
        weigh(0, 1)
        weigh(0, 2)
        quantize_w(0, 0)
        mask_times_t(1)
        weigh(0, 3)

        exp(1, 0)
        pack(nc.scalar.copy, q_bf[2][:], q_raw[2][:])
        weigh(1, 0)
        quantize_w(0, 1)
        quantize_q(2)
        for g in range(1, H):
            exp(1, g)
        scores(2, by_head)
        weigh(1, 1)
        weigh(1, 2)
        quantize_w(1, 0)
        mask_times_t(2)
        weigh(1, 3)

        exp(2, 0)
        pack_v(nc.scalar.copy, 0)
        exp(2, 1)
        pack_v(nc.scalar.copy, 1)
        exp(2, 2)
        exp(2, 3)
        scores(3, by_head)
        weigh(2, 0)
        quantize_w(1, 1)
        pack_v(nc.vector.tensor_copy, 2)
        weigh(2, 1)
        quantize_v(0)
        weigh(2, 2)
        quantize_w(2, 0)
        weigh(2, 3)

        pack_v(nc.scalar.copy, 3)
        for g in range(H):
            exp(3, g)
        for b in range(NT):
            step = 2 if b in (0, NT - 1) else H
            for g0 in range(0, H, step):
                nc.scalar.activation(
                    out=gate[b][:, g0 : g0 + step, :], in_=og_raw[b][:, g0 : g0 + step, :], func=ACT.Sigmoid
                )
        quantize_v(1)
        weigh(3, 0)
        quantize_w(2, 1)
        for b in range(3):
            values(b, range(H))
        weigh(3, 1)
        weigh(3, 2)
        quantize_w(3, 0)
        values(3, range(2))
        weigh(3, 3)
        for b in range(3):
            denominators(b)
        quantize_w(3, 1)
        values(3, range(2, H))
        finish(0, range(H))
        finish(1, range(H))
        denominators(3)
        finish(2, range(H))
        finish(3, range(0, 2))
        finish(3, range(2, H))
